import numpy as np
import ml_dtypes


def mxq(x, axis, fmt="e4m3"):
    dtype, down = {"e4m3": (ml_dtypes.float8_e4m3fn, 7), "e5m2": (ml_dtypes.float8_e5m2, 14)}[fmt]
    v = np.moveaxis(np.asarray(x, np.float32).astype(ml_dtypes.bfloat16).astype(np.float64), axis, -1)
    blocks = v.reshape(v.shape[:-1] + (-1, 32))
    amax = np.abs(blocks).max(-1, keepdims=True)
    byte = np.maximum(np.where(amax > 0, np.frexp(amax)[1] - 1 + 127, 0) - down, 1)
    scale = np.exp2(byte - 127.0)
    codes = (blocks / scale).astype(np.float32).astype(dtype).astype(np.float64)
    return np.moveaxis((codes * scale).reshape(v.shape), -1, axis)


WIDE = False


def mx_kscale(k):
    if not WIDE:
        return np.ones(k)
    levels = np.array([10, -10, 5, -5, 0])
    if k % 512:
        return np.exp2(np.random.permutation(np.resize(levels, k // 32))).repeat(32)
    a = np.empty((k // 512, 16))
    for p in range(k // 512):
        a[p, :8] = np.random.permutation(np.resize(levels, 8))
        for g in range(8):
            far = levels[np.abs(levels - a[p, g]) >= 10]
            a[p, g + 8] = far[np.random.randint(len(far))]
    return np.exp2(a.ravel()).repeat(32)


def f64(x):
    return np.asarray(x).astype(np.float64)


def striped(idx):
    return np.tile(np.asarray(idx).reshape(-1, 16).T, (8, 1)).astype(np.uint16)


def unstriped(offs):
    return offs[:16].T.reshape(-1).astype(np.int64)


E2M1 = np.array([0.0, 0.5, 1.0, 1.5, 2.0, 3.0, 4.0, 6.0, -0.0, -0.5, -1.0, -1.5, -2.0, -3.0, -4.0, -6.0])


def pack_weight(w, fmt):
    k, n = w.shape
    w = f64(np.asarray(w, np.float32).astype(ml_dtypes.bfloat16)).reshape(k // 32, 32, n)
    amax = np.abs(w).max(1)
    if fmt == "e4m3":
        byte = np.frexp(amax)[1] - 1 + 127 - 7
    else:
        mant, ex = np.frexp(amax / 6.0)
        byte = np.where(mant > 0.5, ex, ex - 1) + 127
    byte = np.clip(np.where(amax > 0, byte, 1), 1, 254)
    scaled = (w * np.exp2(127.0 - byte)[:, None, :]).reshape(k, n).astype(np.float32)
    by_word = np.ascontiguousarray(scaled.reshape(k // 512, 128, 4, n).transpose(0, 1, 3, 2))
    if fmt == "e4m3":
        words = by_word.astype(ml_dtypes.float8_e4m3fn).view(np.uint8)
    else:
        c = by_word.astype(ml_dtypes.float4_e2m1fn).view(np.uint8) & 0xF
        words = (c[..., 0::2] | (c[..., 1::2] << 4)).reshape(k // 512, 128, 2 * n)
    return np.ascontiguousarray(words), np.ascontiguousarray(byte.astype(np.uint8).reshape(k // 512, 16, n))


def unpack_weight(words, scales, fmt):
    g, _, n = scales.shape
    words = np.ascontiguousarray(words).reshape(g, 128, n, -1)
    if fmt == "e4m3":
        vals = words.view(ml_dtypes.float8_e4m3fn).astype(np.float64)
    else:
        nib = np.empty((g, 128, n, 4), np.uint8)
        nib[..., 0::2] = words & 0xF
        nib[..., 1::2] = words >> 4
        vals = E2M1[nib]
    vals = vals * np.repeat(np.exp2(scales.astype(np.float64) - 127.0), 8, axis=1)[..., None]
    return vals.transpose(0, 1, 3, 2).reshape(g * 512, n)


def e4m3fn_bytes(y):
    return np.clip(np.asarray(y, np.float64), -448.0, 448.0).astype(np.float32).astype(ml_dtypes.float8_e4m3fn).view(np.uint8)


def e4m3fn_values(b):
    return np.asarray(b, np.uint8).view(ml_dtypes.float8_e4m3fn).astype(np.float64)


K, T, J, R, F, Z, D, N, E = 512, 1024, 256, 512, 512, 1024, 2048, 256, 512


def setup_inputs():
    n = np.random.standard_normal
    idx = np.random.permutation(T)[:J]
    idx2 = np.random.permutation(Z)[:J]
    idx3 = np.random.permutation(E)[:J]
    idx4 = np.random.permutation(D)[:E]
    fk = mx_kscale(K)
    ff = mx_kscale(F)
    fr = mx_kscale(R)
    xtp = pack_weight(n((K, T)) / fk[:, None], "e2m1")
    xop = pack_weight(n((F, Z)) / ff[:, None], "e4m3")
    wp = pack_weight(n((K, R)) * 1 / np.sqrt(K) * fk[:, None] * fr, "e4m3")
    w0p = pack_weight(n((F, R)) * 1 / np.sqrt(F) * ff[:, None] * fr, "e2m1")
    wbp = pack_weight(n((R, N)) * 1 / np.sqrt(R) / fr[:, None], "e2m1")
    return {
        "xt_words": xtp[0],
        "xt_scales": xtp[1],
        "xo_words": xop[0],
        "xo_scales": xop[1],
        "w_words": wp[0],
        "w_scales": wp[1],
        "w0_words": w0p[0],
        "w0_scales": w0p[1],
        "wb_words": wbp[0],
        "wb_scales": wbp[1],
        "so": (np.random.uniform(0.5, 1.6, (N, 1))).astype(np.float32),
        "ca": e4m3fn_bytes(60.0 * n((N, D))),
        "sm": (np.random.uniform(0.004, 0.012, (N, 1))).astype(np.float32),
        "offs": striped(idx),
        "offs2": striped(idx2),
        "offs3": striped(idx3),
        "offs4": striped(idx4),
    }


def reference(xt_words, xt_scales, xo_words, xo_scales, w_words, w_scales, w0_words, w0_scales, wb_words, wb_scales, so, ca, sm, offs, offs2, offs3, offs4):
    idx = unstriped(offs)
    idx2 = unstriped(offs2)
    idx3 = unstriped(offs3)
    idx4 = unstriped(offs4)
    xtu = unpack_weight(xt_words, xt_scales, "e2m1")
    xou = unpack_weight(xo_words, xo_scales, "e4m3")
    wu = unpack_weight(w_words, w_scales, "e4m3")
    w0u = unpack_weight(w0_words, w0_scales, "e2m1")
    wbu = unpack_weight(wb_words, wb_scales, "e2m1")
    xtidxg = xtu[:, idx]
    xoidx2g = xou[:, idx2]
    a = wu.T @ xtidxg + w0u.T @ xoidx2g
    hid = np.maximum(a, 0.0)
    hidq = mxq(hid, 0, "e4m3")
    p = wbu.T @ hidq
    pe = np.zeros((N, E))
    pe[:, idx3] = p * f64(so)
    g1 = e4m3fn_values(ca)[:, idx4] * f64(sm)
    y = np.abs(pe - g1)
    return y

@@ -1,0 +1,158 @@
+from contextlib import ExitStack
+
+import concourse.mybir as mybir
+
+K, T, J, R, F, Z, D, N, E = 512, 1024, 256, 512, 512, 1024, 2048, 256, 512
+FLOPS = 2 * K * R * J + 2 * F * R * J + 2 * R * N * J
+
+F32 = mybir.dt.float32
+BF16 = mybir.dt.bfloat16
+I32 = mybir.dt.int32
+U32 = mybir.dt.uint32
+U16 = mybir.dt.uint16
+U8 = mybir.dt.uint8
+FP8 = mybir.dt.float8_e4m3fn
+FP8X4 = mybir.dt.float8_e4m3fn_x4
+FP4X4 = mybir.dt.float4_e2m1fn_x4
+ACT = mybir.ActivationFunctionType
+ALU = mybir.AluOpType
+
+P = 128
+PACK = 4
+QUADS = 4
+HALF = 128
+EH = E // 2
+
+
+def tile_list_maskedpage_kernel(tc, xt_words, xt_scales, xo_words, xo_scales, w_words, w_scales,
+                                     w0_words, w0_scales, wb_words, wb_scales, so, ca, sm,
+                                     offs, offs2, offs3, offs4, out):
+    nc = tc.nc
+    with ExitStack() as ctx:
+        sb = ctx.enter_context(tc.tile_pool(name="sb", bufs=1))
+        ps = ctx.enter_context(tc.psum_pool(name="ps", bufs=1))
+
+        def tile(shape, dtype, name, tag=None):
+            return sb.tile(shape, dtype, name=name, tag=tag or name, align_bytes=64)
+
+        def load_quadrant(engine, plane, scales, q):
+            engine.dma_start(plane[32 * q : 32 * q + 4, :].bitcast(I32), scales[0, 4 * q : 4 * q + 4, :].bitcast(I32))
+
+        list_t = tile([P, J // 16], U16, "list_t")
+        list_z = tile([P, J // 16], U16, "list_z")
+        list_e = tile([P, J // 16], U16, "list_e")
+        list_d = tile([P, E // 16], U16, "list_d")
+        xt_w = tile([P, T], U16, "xt_w")
+        xo_w = tile([P, Z], U32, "xo_w")
+        xt_s = tile([P, T], U8, "xt_s")
+        xo_s = tile([P, Z], U8, "xo_s")
+        w_w = tile([P, R], U32, "w_w")
+        w0_w = tile([P, R], U16, "w0_w")
+        wb_w = tile([P, N], U16, "wb_w")
+        wb_s = tile([P, N], U8, "wb_s")
+        stage = tile([P, 2, 2 * R], U8, "stage")
+        so_t = tile([P, 2], F32, "so_t")
+        sm_t = tile([P, 2], F32, "sm_t")
+        old = [tile([P, D], U8, "old%d" % n) for n in range(2)]
+        page = [tile([P, E], F32, "page%d" % n) for n in range(2)]
+
+        nc.vector.memset(stage[:].rearrange("p a c -> p (a c)").bitcast(I32), 0)
+        nc.vector.memset(xt_s[:].bitcast(I32), 0)
+        nc.vector.memset(xo_s[:].bitcast(I32), 0)
+        nc.vector.memset(wb_s[:].bitcast(I32), 0)
+
+        nc.sync.dma_start(list_t[:], offs)
+        nc.sync.dma_start(list_z[:], offs2)
+        for i, scales in enumerate((w_scales, w0_scales)):
+            rows = scales[0].rearrange("(a g r) c -> g r a c", a=2, g=2)
+            for g in range(2):
+                nc.scalar.dma_start(stage[32 * g : 32 * g + 4, :, i * R : (i + 1) * R].bitcast(I32), rows[g].bitcast(I32))
+        nc.sync.dma_start(xt_w[:].bitcast(I32), xt_words[0].bitcast(I32))
+        nc.sync.dma_start(xo_w[:].bitcast(I32), xo_words[0].rearrange("p n t -> p (n t)").bitcast(I32))
+        load_quadrant(nc.gpsimd, xo_s, xo_scales, 3)
+        nc.gpsimd.dma_start(w_w[:].bitcast(I32), w_words[0].rearrange("p n t -> p (n t)").bitcast(I32))
+        nc.gpsimd.dma_start(w0_w[:].bitcast(I32), w0_words[0].bitcast(I32))
+        for q in range(QUADS):
+            load_quadrant(nc.scalar, xt_s, xt_scales, q)
+        for q in range(QUADS - 1):
+            load_quadrant(nc.sync, xo_s, xo_scales, q)
+        nc.sync.dma_start(wb_w[:].bitcast(I32), wb_words[0].bitcast(I32))
+        nc.sync.dma_start(list_d[:], offs4)
+        nc.sync.dma_start(old[0][:], ca[0:P, :])
+        for q in range(QUADS):
+            load_quadrant(nc.sync, wb_s, wb_scales, q)
+        nc.sync.dma_start(list_e[:], offs3)
+        nc.sync.dma_start(old[1][:], ca[P : 2 * P, :])
+        with nc.allow_non_contiguous_dma(reason="one value a partition and output half"):
+            nc.gpsimd.dma_start(so_t[:], so.rearrange("(n p) o -> p (n o)", p=P))
+            nc.gpsimd.dma_start(sm_t[:], sm.rearrange("(n p) o -> p (n o)", p=P))
+        for n in range(2):
+            nc.gpsimd.memset(page[n][:], 0.0)
+
+        nc.vector.tensor_copy(stage[64:128, 0, :].bitcast(I32), stage[0:64, 1, :].bitcast(I32))
+        ws = tile([P, 2, PACK, HALF], U8, "ws")
+        nc.vector.tensor_copy(ws[:], stage[:, 0, :].rearrange("p (i m t) -> p i t m", i=2, t=PACK))
+        w_p = tile([P, PACK, HALF], U32, "w_p")
+        nc.scalar.copy(w_p[:].rearrange("p t m -> p m t"), w_w[:].rearrange("p (m t) -> p m t", t=PACK))
+        w0_p = tile([P, PACK, HALF], U16, "w0_p")
+        nc.scalar.copy(w0_p[:], w0_w[:].rearrange("p (m t) -> p t m", t=PACK))
+
+        acc = []
+        for h in range(2):
+            cols = slice(8 * h, 8 * h + 8)
+            gt_w = tile([P, HALF], U16, "gt_w%d" % h)
+            gt_s = tile([P, HALF], U8, "gt_s%d" % h)
+            go_w = tile([P, HALF], U32, "go_w%d" % h)
+            go_s = tile([P, HALF], U8, "go_s%d" % h)
+            nc.vector.tensor_copy(gt_w[:], xt_w[:].indirect(list_t[:, cols]))
+            nc.vector.tensor_copy(gt_s[:], xt_s[:].indirect(list_t[:, cols]))
+            nc.vector.tensor_copy(go_w[:], xo_w[:].indirect(list_z[:, cols]))
+            nc.vector.tensor_copy(go_s[:], xo_s[:].indirect(list_z[:, cols]))
+            a = ps.tile([P, PACK, HALF], F32, name="acc%d" % h)
+            for t in range(PACK):
+                nc.tensor.matmul_mx(out=a[:, t, :], lhsT=w_p[:, t, :].bitcast(FP8X4), lhsT_scale=ws[:, 0, t, :],
+                                    rhs=gt_w[:].bitcast(FP4X4), rhs_scale=gt_s[:], start=(t == 0), stop=False)
+            for t in range(PACK):
+                nc.tensor.matmul_mx(out=a[:, t, :], lhsT=w0_p[:, t, :].bitcast(FP4X4), lhsT_scale=ws[:, 1, t, :],
+                                    rhs=go_w[:].bitcast(FP8X4), rhs_scale=go_s[:], start=False, stop=(t == PACK - 1))
+            acc.append(a)
+
+        p_sb = {}
+        for h in range(2):
+            hid = tile([P, HALF, PACK], BF16, "hid%d" % h)
+            nc.scalar.activation(hid[:], acc[h][:].rearrange("p t j -> p j t"), ACT.Relu)
+            hq_w = tile([P, HALF], U32, "hq_w%d" % h)
+            hq_s = tile([P, HALF], U8, "hq_s%d" % h)
+            nc.vector.quantize_mx(out=hq_w[:].bitcast(FP8X4), scales=hq_s[:], in_=hid[:].rearrange("p j t -> p (j t)"))
+            for n in range(2):
+                ncols = slice(n * HALF, (n + 1) * HALF)
+                prod = ps.tile([P, HALF], F32, name="prod%d%d" % (h, n))
+                nc.tensor.matmul_mx(out=prod[:], lhsT=wb_w[:, ncols].bitcast(FP4X4), lhsT_scale=wb_s[:, ncols],
+                                    rhs=hq_w[:].bitcast(FP8X4), rhs_scale=hq_s[:], start=True, stop=True)
+                p_sb[h, n] = tile([P, HALF], F32, "p_sb%d%d" % (h, n))
+                nc.vector.tensor_copy(p_sb[h, n][:], prod[:])
+
+        for h in range(2):
+            for n in range(2):
+                nc.scalar.activation(page[n][:].indirect(list_e[:, 8 * h : 8 * h + 8]), p_sb[h, n][:], ACT.Copy,
+                                     scale=so_t[:, n : n + 1])
+
+        g1 = [tile([P, E], F32, "g1_%d" % n) for n in range(2)]
+        for n in range(2):
+            for u in range(2):
+                picked = tile([P, EH], U8, "picked%d%d" % (n, u), tag=("hid%d", "hq_w%d")[u] % n)
+                nc.vector.tensor_copy(picked[:], old[n][:].indirect(list_d[:, 16 * u : 16 * u + 16]))
+                nc.vector.tensor_scalar(g1[n][:, u * EH : (u + 1) * EH], picked[:].bitcast(FP8), sm_t[:, n : n + 1], None, ALU.mult)
+
+        diff = [tile([P, E], F32, "diff%d" % n) for n in range(2)]
+        res = [tile([P, E], F32, "res%d" % n) for n in range(2)]
+        nc.vector.tensor_tensor(diff[0][:], page[0][:], g1[0][:], ALU.subtract)
+        for u in range(2):
+            ecols = slice(u * EH, (u + 1) * EH)
+            nc.vector.tensor_tensor(diff[1][:, ecols], page[1][:, ecols], g1[1][:, ecols], ALU.subtract)
+        nc.scalar.activation(res[0][:], diff[0][:], ACT.Abs)
+        nc.sync.dma_start(out[0:P, :], res[0][:])
+        nc.scalar.activation(res[1][:, 0:EH], diff[1][:, 0:EH], ACT.Abs)
+        nc.sync.dma_start(out[P : 2 * P, 0:EH], res[1][:, 0:EH])
+        nc.vector.scalar_tensor_tensor(res[1][:, EH:E], diff[1][:, EH:E], -1.0, diff[1][:, EH:E], ALU.mult, ALU.max)
+        nc.sync.dma_start(out[P : 2 * P, EH:E], res[1][:, EH:E])

@@ -48,54 +48,53 @@ def tile_list_maskedpage_kernel(tc, xt_words, xt_scales, xo_words, xo_scales, w_
         xo_s = tile([P, Z], U8, "xo_s")
         w_w = tile([P, R], U32, "w_w")
         w0_w = tile([P, R], U16, "w0_w")
-        wb_w = tile([P, N], U16, "wb_w")
         wb_s = tile([P, N], U8, "wb_s")
-        stage = tile([P, 2, 2 * R], U8, "stage")
-        so_t = tile([P, 2], F32, "so_t")
+        stage = tile([4, QUADS, 2 * R], U8, "stage")
+        spread = tile([P, 2 * R], U8, "spread")
         sm_t = tile([P, 2], F32, "sm_t")
-        old = [tile([P, D], U8, "old%d" % n) for n in range(2)]
         page = [tile([P, E], F32, "page%d" % n) for n in range(2)]
 
-        nc.vector.memset(stage[:].rearrange("p a c -> p (a c)").bitcast(I32), 0)
-        nc.vector.memset(xt_s[:].bitcast(I32), 0)
-        nc.vector.memset(xo_s[:].bitcast(I32), 0)
+        nc.gpsimd.memset(xt_s[:].bitcast(I32), 0)
+        nc.gpsimd.memset(xo_s[:].bitcast(I32), 0)
+        nc.vector.memset(spread[:].bitcast(I32), 0)
         nc.vector.memset(wb_s[:].bitcast(I32), 0)
+        for n in range(2):
+            nc.vector.memset(page[n][:], 0.0)
 
         nc.sync.dma_start(list_t[:], offs)
         nc.sync.dma_start(list_z[:], offs2)
         for i, scales in enumerate((w_scales, w0_scales)):
-            rows = scales[0].rearrange("(a g r) c -> g r a c", a=2, g=2)
-            for g in range(2):
-                nc.scalar.dma_start(stage[32 * g : 32 * g + 4, :, i * R : (i + 1) * R].bitcast(I32), rows[g].bitcast(I32))
+            rows = scales[0].rearrange("(q r) c -> r q c", r=4)
+            nc.sync.dma_start(stage[:, :, i * R : (i + 1) * R].bitcast(I32), rows.bitcast(I32))
         nc.sync.dma_start(xt_w[:].bitcast(I32), xt_words[0].bitcast(I32))
         nc.sync.dma_start(xo_w[:].bitcast(I32), xo_words[0].rearrange("p n t -> p (n t)").bitcast(I32))
-        load_quadrant(nc.gpsimd, xo_s, xo_scales, 3)
         nc.gpsimd.dma_start(w_w[:].bitcast(I32), w_words[0].rearrange("p n t -> p (n t)").bitcast(I32))
         nc.gpsimd.dma_start(w0_w[:].bitcast(I32), w0_words[0].bitcast(I32))
         for q in range(QUADS):
-            load_quadrant(nc.scalar, xt_s, xt_scales, q)
-        for q in range(QUADS - 1):
+            load_quadrant(nc.sync, xt_s, xt_scales, q)
+        for q in range(QUADS):
             load_quadrant(nc.sync, xo_s, xo_scales, q)
-        nc.sync.dma_start(wb_w[:].bitcast(I32), wb_words[0].bitcast(I32))
         nc.sync.dma_start(list_d[:], offs4)
-        nc.sync.dma_start(old[0][:], ca[0:P, :])
+        nc.sync.dma_start(list_e[:], offs3)
         for q in range(QUADS):
             load_quadrant(nc.sync, wb_s, wb_scales, q)
-        nc.sync.dma_start(list_e[:], offs3)
-        nc.sync.dma_start(old[1][:], ca[P : 2 * P, :])
         with nc.allow_non_contiguous_dma(reason="one value a partition and output half"):
-            nc.gpsimd.dma_start(so_t[:], so.rearrange("(n p) o -> p (n o)", p=P))
             nc.gpsimd.dma_start(sm_t[:], sm.rearrange("(n p) o -> p (n o)", p=P))
-        for n in range(2):
-            nc.gpsimd.memset(page[n][:], 0.0)
 
-        nc.vector.tensor_copy(stage[64:128, 0, :].bitcast(I32), stage[0:64, 1, :].bitcast(I32))
+        for q in range(QUADS):
+            nc.vector.tensor_copy(spread[32 * q : 32 * q + 4, :].bitcast(I32), stage[:, q, :].bitcast(I32))
         ws = tile([P, 2, PACK, HALF], U8, "ws")
-        nc.vector.tensor_copy(ws[:], stage[:, 0, :].rearrange("p (i m t) -> p i t m", i=2, t=PACK))
+        nc.vector.tensor_copy(ws[:], spread[:].rearrange("p (i m t) -> p i t m", i=2, t=PACK))
         w_p = tile([P, PACK, HALF], U32, "w_p")
         nc.scalar.copy(w_p[:].rearrange("p t m -> p m t"), w_w[:].rearrange("p (m t) -> p m t", t=PACK))
         w0_p = tile([P, PACK, HALF], U16, "w0_p")
         nc.scalar.copy(w0_p[:], w0_w[:].rearrange("p (m t) -> p t m", t=PACK))
+
+        wb_w = tile([P, N], U16, "wb_w", tag="stage")
+        nc.sync.dma_start(wb_w[:].bitcast(I32), wb_words[0].bitcast(I32))
+        old = [tile([P, D], U8, "old%d" % n, tag=("spread", "w_w")[n]) for n in range(2)]
+        for n in range(2):
+            nc.sync.dma_start(old[n][:], ca[n * P : (n + 1) * P, :])
 
         acc = []
         for h in range(2):
@@ -117,6 +116,10 @@ def tile_list_maskedpage_kernel(tc, xt_words, xt_scales, xo_words, xo_scales, w_
                                     rhs=go_w[:].bitcast(FP8X4), rhs_scale=go_s[:], start=False, stop=(t == PACK - 1))
             acc.append(a)
 
+        so_t = tile([P, 2], F32, "so_t", tag="xt_w")
+        with nc.allow_non_contiguous_dma(reason="one value a partition and output half"):
+            nc.sync.dma_start(so_t[:], so.rearrange("(n p) o -> p (n o)", p=P))
+
         p_sb = {}
         for h in range(2):
             hid = tile([P, HALF, PACK], BF16, "hid%d" % h)
@@ -124,25 +127,24 @@ def tile_list_maskedpage_kernel(tc, xt_words, xt_scales, xo_words, xo_scales, w_
             hq_w = tile([P, HALF], U32, "hq_w%d" % h)
             hq_s = tile([P, HALF], U8, "hq_s%d" % h)
             nc.vector.quantize_mx(out=hq_w[:].bitcast(FP8X4), scales=hq_s[:], in_=hid[:].rearrange("p j t -> p (j t)"))
+            prod = ps.tile([P, 2, HALF], F32, name="prod%d" % h)
             for n in range(2):
                 ncols = slice(n * HALF, (n + 1) * HALF)
-                prod = ps.tile([P, HALF], F32, name="prod%d%d" % (h, n))
-                nc.tensor.matmul_mx(out=prod[:], lhsT=wb_w[:, ncols].bitcast(FP4X4), lhsT_scale=wb_s[:, ncols],
+                nc.tensor.matmul_mx(out=prod[:, n, :], lhsT=wb_w[:, ncols].bitcast(FP4X4), lhsT_scale=wb_s[:, ncols],
                                     rhs=hq_w[:].bitcast(FP8X4), rhs_scale=hq_s[:], start=True, stop=True)
-                p_sb[h, n] = tile([P, HALF], F32, "p_sb%d%d" % (h, n))
-                nc.vector.tensor_copy(p_sb[h, n][:], prod[:])
+            p_sb[h] = tile([P, 2, HALF], F32, "p_sb%d" % h)
+            nc.scalar.copy(p_sb[h][:], prod[:])
 
         for h in range(2):
             for n in range(2):
-                nc.scalar.activation(page[n][:].indirect(list_e[:, 8 * h : 8 * h + 8]), p_sb[h, n][:], ACT.Copy,
+                nc.scalar.activation(page[n][:].indirect(list_e[:, 8 * h : 8 * h + 8]), p_sb[h][:, n, :], ACT.Copy,
                                      scale=so_t[:, n : n + 1])
 
         g1 = [tile([P, E], F32, "g1_%d" % n) for n in range(2)]
         for n in range(2):
-            for u in range(2):
-                picked = tile([P, EH], U8, "picked%d%d" % (n, u), tag=("hid%d", "hq_w%d")[u] % n)
-                nc.vector.tensor_copy(picked[:], old[n][:].indirect(list_d[:, 16 * u : 16 * u + 16]))
-                nc.vector.tensor_scalar(g1[n][:, u * EH : (u + 1) * EH], picked[:].bitcast(FP8), sm_t[:, n : n + 1], None, ALU.mult)
+            picked = tile([P, E], U8, "picked%d" % n, tag="hid%d" % n)
+            nc.vector.tensor_copy(picked[:], old[n][:].indirect(list_d[:]))
+            nc.vector.tensor_scalar(g1[n][:], picked[:].bitcast(FP8), sm_t[:, n : n + 1], None, ALU.mult)
 
         diff = [tile([P, E], F32, "diff%d" % n) for n in range(2)]
         res = [tile([P, E], F32, "res%d" % n) for n in range(2)]

@@ -48,53 +48,55 @@ def tile_list_maskedpage_kernel(tc, xt_words, xt_scales, xo_words, xo_scales, w_
         xo_s = tile([P, Z], U8, "xo_s")
         w_w = tile([P, R], U32, "w_w")
         w0_w = tile([P, R], U16, "w0_w")
-        wb_s = tile([P, N], U8, "wb_s")
-        stage = tile([4, QUADS, 2 * R], U8, "stage")
-        spread = tile([P, 2 * R], U8, "spread")
+        wb_w = tile([P, N], U16, "wb_w")
+        wb_s = tile([P, 2, N], U8, "wb_s")
+        so_t = tile([P, 2], F32, "so_t")
         sm_t = tile([P, 2], F32, "sm_t")
+        stage = tile([P, 2, 2 * R], U8, "stage")
+        old = [tile([P, D], U8, "old%d" % n) for n in range(2)]
         page = [tile([P, E], F32, "page%d" % n) for n in range(2)]
 
+        nc.gpsimd.memset(stage[:].rearrange("p a c -> p (a c)").bitcast(I32), 0)
         nc.gpsimd.memset(xt_s[:].bitcast(I32), 0)
         nc.gpsimd.memset(xo_s[:].bitcast(I32), 0)
-        nc.vector.memset(spread[:].bitcast(I32), 0)
-        nc.vector.memset(wb_s[:].bitcast(I32), 0)
+        nc.vector.memset(wb_s[:].rearrange("p a c -> p (a c)").bitcast(I32), 0)
         for n in range(2):
-            nc.vector.memset(page[n][:], 0.0)
+            nc.vector.memset(page[n][:, 0 : EH + 1], 0.0)
+            nc.vector.memset(page[n][:, EH + 1 : E], 0.0)
+
+        def load_staged(engine, dest, scales):
+            rows = scales[0].rearrange("(a g r) c -> g r a c", a=2, g=2)
+            for g in range(2):
+                engine.dma_start(dest[32 * g : 32 * g + 4].bitcast(I32), rows[g].bitcast(I32))
 
         nc.sync.dma_start(list_t[:], offs)
         nc.sync.dma_start(list_z[:], offs2)
-        for i, scales in enumerate((w_scales, w0_scales)):
-            rows = scales[0].rearrange("(q r) c -> r q c", r=4)
-            nc.sync.dma_start(stage[:, :, i * R : (i + 1) * R].bitcast(I32), rows.bitcast(I32))
+        load_staged(nc.scalar, stage[:, :, 0:R], w_scales)
+        load_staged(nc.sync, stage[:, :, R : 2 * R], w0_scales)
         nc.sync.dma_start(xt_w[:].bitcast(I32), xt_words[0].bitcast(I32))
         nc.sync.dma_start(xo_w[:].bitcast(I32), xo_words[0].rearrange("p n t -> p (n t)").bitcast(I32))
         nc.gpsimd.dma_start(w_w[:].bitcast(I32), w_words[0].rearrange("p n t -> p (n t)").bitcast(I32))
         nc.gpsimd.dma_start(w0_w[:].bitcast(I32), w0_words[0].bitcast(I32))
-        for q in range(QUADS):
-            load_quadrant(nc.sync, xt_s, xt_scales, q)
-        for q in range(QUADS):
-            load_quadrant(nc.sync, xo_s, xo_scales, q)
+        nc.gpsimd.dma_start(wb_w[:].bitcast(I32), wb_words[0].bitcast(I32))
+        for plane, scales in ((xt_s, xt_scales), (xo_s, xo_scales)):
+            for q in range(QUADS):
+                load_quadrant(nc.sync, plane, scales, q)
+        load_staged(nc.sync, wb_s[:], wb_scales)
         nc.sync.dma_start(list_d[:], offs4)
+        nc.sync.dma_start(old[0][:], ca[0:P, :])
         nc.sync.dma_start(list_e[:], offs3)
-        for q in range(QUADS):
-            load_quadrant(nc.sync, wb_s, wb_scales, q)
         with nc.allow_non_contiguous_dma(reason="one value a partition and output half"):
-            nc.gpsimd.dma_start(sm_t[:], sm.rearrange("(n p) o -> p (n o)", p=P))
+            nc.sync.dma_start(so_t[:], so.rearrange("(n p) o -> p (n o)", p=P))
+            nc.sync.dma_start(old[1][:], ca[P : 2 * P, :])
+            nc.sync.dma_start(sm_t[:], sm.rearrange("(n p) o -> p (n o)", p=P))
 
-        for q in range(QUADS):
-            nc.vector.tensor_copy(spread[32 * q : 32 * q + 4, :].bitcast(I32), stage[:, q, :].bitcast(I32))
+        nc.vector.tensor_copy(stage[64:128, 0, :].bitcast(I32), stage[0:64, 1, :].bitcast(I32))
         ws = tile([P, 2, PACK, HALF], U8, "ws")
-        nc.vector.tensor_copy(ws[:], spread[:].rearrange("p (i m t) -> p i t m", i=2, t=PACK))
+        nc.vector.tensor_copy(ws[:], stage[:, 0, :].rearrange("p (i m t) -> p i t m", i=2, t=PACK))
         w_p = tile([P, PACK, HALF], U32, "w_p")
         nc.scalar.copy(w_p[:].rearrange("p t m -> p m t"), w_w[:].rearrange("p (m t) -> p m t", t=PACK))
         w0_p = tile([P, PACK, HALF], U16, "w0_p")
         nc.scalar.copy(w0_p[:], w0_w[:].rearrange("p (m t) -> p t m", t=PACK))
-
-        wb_w = tile([P, N], U16, "wb_w", tag="stage")
-        nc.sync.dma_start(wb_w[:].bitcast(I32), wb_words[0].bitcast(I32))
-        old = [tile([P, D], U8, "old%d" % n, tag=("spread", "w_w")[n]) for n in range(2)]
-        for n in range(2):
-            nc.sync.dma_start(old[n][:], ca[n * P : (n + 1) * P, :])
 
         acc = []
         for h in range(2):
@@ -116,11 +118,8 @@ def tile_list_maskedpage_kernel(tc, xt_words, xt_scales, xo_words, xo_scales, w_
                                     rhs=go_w[:].bitcast(FP8X4), rhs_scale=go_s[:], start=False, stop=(t == PACK - 1))
             acc.append(a)
 
-        so_t = tile([P, 2], F32, "so_t", tag="xt_w")
-        with nc.allow_non_contiguous_dma(reason="one value a partition and output half"):
-            nc.sync.dma_start(so_t[:], so.rearrange("(n p) o -> p (n o)", p=P))
-
-        p_sb = {}
+        nc.vector.tensor_copy(wb_s[64:128, 0, :].bitcast(I32), wb_s[0:64, 1, :].bitcast(I32))
+        prods = []
         for h in range(2):
             hid = tile([P, HALF, PACK], BF16, "hid%d" % h)
             nc.scalar.activation(hid[:], acc[h][:].rearrange("p t j -> p j t"), ACT.Relu)
@@ -130,21 +129,22 @@ def tile_list_maskedpage_kernel(tc, xt_words, xt_scales, xo_words, xo_scales, w_
             prod = ps.tile([P, 2, HALF], F32, name="prod%d" % h)
             for n in range(2):
                 ncols = slice(n * HALF, (n + 1) * HALF)
-                nc.tensor.matmul_mx(out=prod[:, n, :], lhsT=wb_w[:, ncols].bitcast(FP4X4), lhsT_scale=wb_s[:, ncols],
+                nc.tensor.matmul_mx(out=prod[:, n, :], lhsT=wb_w[:, ncols].bitcast(FP4X4), lhsT_scale=wb_s[:, 0, ncols],
                                     rhs=hq_w[:].bitcast(FP8X4), rhs_scale=hq_s[:], start=True, stop=True)
-            p_sb[h] = tile([P, 2, HALF], F32, "p_sb%d" % h)
-            nc.scalar.copy(p_sb[h][:], prod[:])
+            prods.append(prod)
 
         for h in range(2):
+            p_sb = tile([P, 2, HALF], F32, "p_sb%d" % h)
+            (nc.scalar.copy, nc.vector.tensor_copy)[h](p_sb[:], prods[h][:])
             for n in range(2):
-                nc.scalar.activation(page[n][:].indirect(list_e[:, 8 * h : 8 * h + 8]), p_sb[h][:, n, :], ACT.Copy,
+                nc.scalar.activation(page[n][:].indirect(list_e[:, 8 * h : 8 * h + 8]), p_sb[:, n, :], ACT.Copy,
                                      scale=so_t[:, n : n + 1])
 
         g1 = [tile([P, E], F32, "g1_%d" % n) for n in range(2)]
-        for n in range(2):
-            picked = tile([P, E], U8, "picked%d" % n, tag="hid%d" % n)
-            nc.vector.tensor_copy(picked[:], old[n][:].indirect(list_d[:]))
-            nc.vector.tensor_scalar(g1[n][:], picked[:].bitcast(FP8), sm_t[:, n : n + 1], None, ALU.mult)
+        for n, first, last, tag in ((0, 0, EH, "hid0"), (0, EH, E, "hid1"), (1, 0, E, "hq_w1")):
+            picked = tile([P, last - first], U8, "picked%d_%d" % (n, first), tag=tag)
+            nc.vector.tensor_copy(picked[:], old[n][:].indirect(list_d[:, first // 16 : last // 16]))
+            nc.vector.tensor_scalar(g1[n][:, first:last], picked[:].bitcast(FP8), sm_t[:, n : n + 1], None, ALU.mult)
 
         diff = [tile([P, E], F32, "diff%d" % n) for n in range(2)]
         res = [tile([P, E], F32, "res%d" % n) for n in range(2)]

from contextlib import ExitStack

import concourse.mybir as mybir

K, T, J, R, F, Z, D, N, E = 512, 1024, 256, 512, 512, 1024, 2048, 256, 512
FLOPS = 2 * K * R * J + 2 * F * R * J + 2 * R * N * J

F32 = mybir.dt.float32
BF16 = mybir.dt.bfloat16
I32 = mybir.dt.int32
U32 = mybir.dt.uint32
U16 = mybir.dt.uint16
U8 = mybir.dt.uint8
FP8 = mybir.dt.float8_e4m3fn
FP8X4 = mybir.dt.float8_e4m3fn_x4
FP4X4 = mybir.dt.float4_e2m1fn_x4
ACT = mybir.ActivationFunctionType
ALU = mybir.AluOpType

P = 128
PACK = 4
QUADS = 4
HALF = 128
EH = E // 2


def tile_list_maskedpage_kernel(tc, xt_words, xt_scales, xo_words, xo_scales, w_words, w_scales,
                                     w0_words, w0_scales, wb_words, wb_scales, so, ca, sm,
                                     offs, offs2, offs3, offs4, out):
    nc = tc.nc
    with ExitStack() as ctx:
        sb = ctx.enter_context(tc.tile_pool(name="sb", bufs=1))
        ps = ctx.enter_context(tc.psum_pool(name="ps", bufs=1))

        def tile(shape, dtype, name, tag=None):
            return sb.tile(shape, dtype, name=name, tag=tag or name, align_bytes=64)

        def load_quadrant(engine, plane, scales, q):
            engine.dma_start(plane[32 * q : 32 * q + 4, :].bitcast(I32), scales[0, 4 * q : 4 * q + 4, :].bitcast(I32))

        list_t = tile([P, J // 16], U16, "list_t")
        list_z = tile([P, J // 16], U16, "list_z")
        list_e = tile([P, J // 16], U16, "list_e")
        list_d = tile([P, E // 16], U16, "list_d")
        xt_w = tile([P, T], U16, "xt_w")
        xo_w = tile([P, Z], U32, "xo_w")
        xt_s = tile([P, T], U8, "xt_s")
        xo_s = tile([P, Z], U8, "xo_s")
        w_w = tile([P, R], U32, "w_w")
        w0_w = tile([P, R], U16, "w0_w")
        wb_w = tile([P, N], U16, "wb_w")
        wb_s = tile([P, 2, N], U8, "wb_s")
        so_t = tile([P, 2], F32, "so_t")
        sm_t = tile([P, 2], F32, "sm_t")
        stage = tile([P, 2, 2 * R], U8, "stage")
        old = [tile([P, D], U8, "old%d" % n) for n in range(2)]
        page = [tile([P, E], F32, "page%d" % n) for n in range(2)]

        nc.gpsimd.memset(stage[:].rearrange("p a c -> p (a c)").bitcast(I32), 0)
        nc.gpsimd.memset(xt_s[:].bitcast(I32), 0)
        nc.gpsimd.memset(xo_s[:].bitcast(I32), 0)
        nc.vector.memset(wb_s[:].rearrange("p a c -> p (a c)").bitcast(I32), 0)
        for n in range(2):
            nc.vector.memset(page[n][:, 0 : EH + 1], 0.0)
            nc.vector.memset(page[n][:, EH + 1 : E], 0.0)

        def load_staged(engine, dest, scales):
            rows = scales[0].rearrange("(a g r) c -> g r a c", a=2, g=2)
            for g in range(2):
                engine.dma_start(dest[32 * g : 32 * g + 4].bitcast(I32), rows[g].bitcast(I32))

        nc.sync.dma_start(list_t[:], offs)
        nc.sync.dma_start(list_z[:], offs2)
        load_staged(nc.scalar, stage[:, :, 0:R], w_scales)
        load_staged(nc.sync, stage[:, :, R : 2 * R], w0_scales)
        nc.sync.dma_start(xt_w[:].bitcast(I32), xt_words[0].bitcast(I32))
        nc.sync.dma_start(xo_w[:].bitcast(I32), xo_words[0].rearrange("p n t -> p (n t)").bitcast(I32))
        nc.gpsimd.dma_start(w_w[:].bitcast(I32), w_words[0].rearrange("p n t -> p (n t)").bitcast(I32))
        nc.gpsimd.dma_start(w0_w[:].bitcast(I32), w0_words[0].bitcast(I32))
        nc.gpsimd.dma_start(wb_w[:].bitcast(I32), wb_words[0].bitcast(I32))
        for plane, scales in ((xt_s, xt_scales), (xo_s, xo_scales)):
            for q in range(QUADS):
                load_quadrant(nc.sync, plane, scales, q)
        load_staged(nc.sync, wb_s[:], wb_scales)
        nc.sync.dma_start(list_d[:], offs4)
        nc.sync.dma_start(old[0][:], ca[0:P, :])
        nc.sync.dma_start(list_e[:], offs3)
        with nc.allow_non_contiguous_dma(reason="one value a partition and output half"):
            nc.sync.dma_start(so_t[:], so.rearrange("(n p) o -> p (n o)", p=P))
            nc.sync.dma_start(old[1][:], ca[P : 2 * P, :])
            nc.sync.dma_start(sm_t[:], sm.rearrange("(n p) o -> p (n o)", p=P))

        nc.vector.tensor_copy(stage[64:128, 0, :].bitcast(I32), stage[0:64, 1, :].bitcast(I32))
        ws = tile([P, 2, PACK, HALF], U8, "ws")
        nc.vector.tensor_copy(ws[:], stage[:, 0, :].rearrange("p (i m t) -> p i t m", i=2, t=PACK))
        w_p = tile([P, PACK, HALF], U32, "w_p")
        nc.scalar.copy(w_p[:].rearrange("p t m -> p m t"), w_w[:].rearrange("p (m t) -> p m t", t=PACK))
        w0_p = tile([P, PACK, HALF], U16, "w0_p")
        nc.scalar.copy(w0_p[:], w0_w[:].rearrange("p (m t) -> p t m", t=PACK))

        acc = []
        for h in range(2):
            cols = slice(8 * h, 8 * h + 8)
            gt_w = tile([P, HALF], U16, "gt_w%d" % h)
            gt_s = tile([P, HALF], U8, "gt_s%d" % h)
            go_w = tile([P, HALF], U32, "go_w%d" % h)
            go_s = tile([P, HALF], U8, "go_s%d" % h)
            nc.vector.tensor_copy(gt_w[:], xt_w[:].indirect(list_t[:, cols]))
            nc.vector.tensor_copy(gt_s[:], xt_s[:].indirect(list_t[:, cols]))
            nc.vector.tensor_copy(go_w[:], xo_w[:].indirect(list_z[:, cols]))
            nc.vector.tensor_copy(go_s[:], xo_s[:].indirect(list_z[:, cols]))
            a = ps.tile([P, PACK, HALF], F32, name="acc%d" % h)
            for t in range(PACK):
                nc.tensor.matmul_mx(out=a[:, t, :], lhsT=w_p[:, t, :].bitcast(FP8X4), lhsT_scale=ws[:, 0, t, :],
                                    rhs=gt_w[:].bitcast(FP4X4), rhs_scale=gt_s[:], start=(t == 0), stop=False)
            for t in range(PACK):
                nc.tensor.matmul_mx(out=a[:, t, :], lhsT=w0_p[:, t, :].bitcast(FP4X4), lhsT_scale=ws[:, 1, t, :],
                                    rhs=go_w[:].bitcast(FP8X4), rhs_scale=go_s[:], start=False, stop=(t == PACK - 1))
            acc.append(a)

        nc.vector.tensor_copy(wb_s[64:128, 0, :].bitcast(I32), wb_s[0:64, 1, :].bitcast(I32))
        prods = []
        for h in range(2):
            hid = tile([P, HALF, PACK], BF16, "hid%d" % h)
            nc.scalar.activation(hid[:], acc[h][:].rearrange("p t j -> p j t"), ACT.Relu)
            hq_w = tile([P, HALF], U32, "hq_w%d" % h)
            hq_s = tile([P, HALF], U8, "hq_s%d" % h)
            nc.vector.quantize_mx(out=hq_w[:].bitcast(FP8X4), scales=hq_s[:], in_=hid[:].rearrange("p j t -> p (j t)"))
            prod = ps.tile([P, 2, HALF], F32, name="prod%d" % h)
            for n in range(2):
                ncols = slice(n * HALF, (n + 1) * HALF)
                nc.tensor.matmul_mx(out=prod[:, n, :], lhsT=wb_w[:, ncols].bitcast(FP4X4), lhsT_scale=wb_s[:, 0, ncols],
                                    rhs=hq_w[:].bitcast(FP8X4), rhs_scale=hq_s[:], start=True, stop=True)
            prods.append(prod)

        for h in range(2):
            p_sb = tile([P, 2, HALF], F32, "p_sb%d" % h)
            (nc.scalar.copy, nc.vector.tensor_copy)[h](p_sb[:], prods[h][:])
            for n in range(2):
                nc.scalar.activation(page[n][:].indirect(list_e[:, 8 * h : 8 * h + 8]), p_sb[:, n, :], ACT.Copy,
                                     scale=so_t[:, n : n + 1])

        g1 = [tile([P, E], F32, "g1_%d" % n) for n in range(2)]
        for n, first, last, tag in ((0, 0, EH, "hid0"), (0, EH, E, "hid1"), (1, 0, E, "hq_w1")):
            picked = tile([P, last - first], U8, "picked%d_%d" % (n, first), tag=tag)
            nc.vector.tensor_copy(picked[:], old[n][:].indirect(list_d[:, first // 16 : last // 16]))
            nc.vector.tensor_scalar(g1[n][:, first:last], picked[:].bitcast(FP8), sm_t[:, n : n + 1], None, ALU.mult)

        diff = [tile([P, E], F32, "diff%d" % n) for n in range(2)]
        res = [tile([P, E], F32, "res%d" % n) for n in range(2)]
        nc.vector.tensor_tensor(diff[0][:], page[0][:], g1[0][:], ALU.subtract)
        for u in range(2):
            ecols = slice(u * EH, (u + 1) * EH)
            nc.vector.tensor_tensor(diff[1][:, ecols], page[1][:, ecols], g1[1][:, ecols], ALU.subtract)
        nc.scalar.activation(res[0][:], diff[0][:], ACT.Abs)
        nc.sync.dma_start(out[0:P, :], res[0][:])
        nc.scalar.activation(res[1][:, 0:EH], diff[1][:, 0:EH], ACT.Abs)
        nc.sync.dma_start(out[P : 2 * P, 0:EH], res[1][:, 0:EH])
        nc.vector.scalar_tensor_tensor(res[1][:, EH:E], diff[1][:, EH:E], -1.0, diff[1][:, EH:E], ALU.mult, ALU.max)
        nc.sync.dma_start(out[P : 2 * P, EH:E], res[1][:, EH:E])
